import numpy as np
import ml_dtypes


def mxq(x, axis, fmt="e4m3"):
    dtype, down = {"e4m3": (ml_dtypes.float8_e4m3fn, 7), "e5m2": (ml_dtypes.float8_e5m2, 14)}[fmt]
    v = np.moveaxis(np.asarray(x, np.float32).astype(ml_dtypes.bfloat16).astype(np.float64), axis, -1)
    blocks = v.reshape(v.shape[:-1] + (-1, 32))
    amax = np.abs(blocks).max(-1, keepdims=True)
    byte = np.maximum(np.where(amax > 0, np.frexp(amax)[1] - 1 + 127, 0) - down, 1)
    scale = np.exp2(byte - 127.0)
    codes = (blocks / scale).astype(np.float32).astype(dtype).astype(np.float64)
    return np.moveaxis((codes * scale).reshape(v.shape), -1, axis)


WIDE = False


def mx_kscale(k):
    if not WIDE:
        return np.ones(k)
    levels = np.array([10, -10, 5, -5, 0])
    if k % 512:
        return np.exp2(np.random.permutation(np.resize(levels, k // 32))).repeat(32)
    a = np.empty((k // 512, 16))
    for p in range(k // 512):
        a[p, :8] = np.random.permutation(np.resize(levels, 8))
        for g in range(8):
            far = levels[np.abs(levels - a[p, g]) >= 10]
            a[p, g + 8] = far[np.random.randint(len(far))]
    return np.exp2(a.ravel()).repeat(32)


def f64(x):
    return np.asarray(x).astype(np.float64)


def striped(idx):
    return np.tile(np.asarray(idx).reshape(-1, 16).T, (8, 1)).astype(np.uint16)


def unstriped(offs):
    return offs[:16].T.reshape(-1).astype(np.int64)


def striped8(idx):
    return np.asarray(idx).reshape(8, -1, 16).transpose(0, 2, 1).reshape(128, -1).astype(np.uint16)


def unstriped8(offs):
    return offs.reshape(8, 16, -1).transpose(0, 2, 1).reshape(8, -1).astype(np.int64)


def pick8(x, idx, run):
    r = np.arange(len(x))
    return x[r[:, None], idx[r % (8 * run) // run]]


E2M1 = np.array([0.0, 0.5, 1.0, 1.5, 2.0, 3.0, 4.0, 6.0, -0.0, -0.5, -1.0, -1.5, -2.0, -3.0, -4.0, -6.0])


def pack_weight(w, fmt):
    k, n = w.shape
    w = f64(np.asarray(w, np.float32).astype(ml_dtypes.bfloat16)).reshape(k // 32, 32, n)
    amax = np.abs(w).max(1)
    if fmt == "e4m3":
        byte = np.frexp(amax)[1] - 1 + 127 - 7
    else:
        mant, ex = np.frexp(amax / 6.0)
        byte = np.where(mant > 0.5, ex, ex - 1) + 127
    byte = np.clip(np.where(amax > 0, byte, 1), 1, 254)
    scaled = (w * np.exp2(127.0 - byte)[:, None, :]).reshape(k, n).astype(np.float32)
    by_word = np.ascontiguousarray(scaled.reshape(k // 512, 128, 4, n).transpose(0, 1, 3, 2))
    if fmt == "e4m3":
        words = by_word.astype(ml_dtypes.float8_e4m3fn).view(np.uint8)
    else:
        c = by_word.astype(ml_dtypes.float4_e2m1fn).view(np.uint8) & 0xF
        words = (c[..., 0::2] | (c[..., 1::2] << 4)).reshape(k // 512, 128, 2 * n)
    return np.ascontiguousarray(words), np.ascontiguousarray(byte.astype(np.uint8).reshape(k // 512, 16, n))


def unpack_weight(words, scales, fmt):
    g, _, n = scales.shape
    words = np.ascontiguousarray(words).reshape(g, 128, n, -1)
    if fmt == "e4m3":
        vals = words.view(ml_dtypes.float8_e4m3fn).astype(np.float64)
    else:
        nib = np.empty((g, 128, n, 4), np.uint8)
        nib[..., 0::2] = words & 0xF
        nib[..., 1::2] = words >> 4
        vals = E2M1[nib]
    vals = vals * np.repeat(np.exp2(scales.astype(np.float64) - 127.0), 8, axis=1)[..., None]
    return vals.transpose(0, 1, 3, 2).reshape(g * 512, n)


K, J, R, T, C, N, S, U = 512, 256, 512, 1024, 512, 256, 1024, 1024


def setup_inputs():
    n = np.random.standard_normal
    idx = np.random.permutation(T)[:J]
    idx2 = np.stack([np.random.permutation(C)[:J] for _ in range(8)])
    idx3 = np.stack([np.random.permutation(C)[:J] for _ in range(8)])
    idx4 = np.random.permutation(S)[:N]
    idx5 = np.stack([np.random.permutation(U)[:C] for _ in range(8)])
    idx6 = np.stack([np.random.permutation(U)[:C] for _ in range(8)])
    idx7 = np.stack([np.random.permutation(U)[:C] for _ in range(8)])
    fk = mx_kscale(K)
    fr = mx_kscale(R)
    xtp = pack_weight(n((K, T)) * fk[:, None], "e4m3")
    wp = pack_weight(n((K, R)) * 1 / np.sqrt(K) / fk[:, None], "e4m3")
    w2p = pack_weight(n((K, R)) * 1 / np.sqrt(K) / fk[:, None], "e2m1")
    vsp = pack_weight(n((R, S)) * 1 / np.sqrt(R) / fr[:, None], "e2m1")
    return {
        "xt_words": xtp[0],
        "xt_scales": xtp[1],
        "w_words": wp[0],
        "w_scales": wp[1],
        "w2_words": w2p[0],
        "w2_scales": w2p[1],
        "sa": (np.random.uniform(0.5, 1.6, (R, 1)) * fr[:, None]).astype(np.float32),
        "vs_words": vsp[0],
        "vs_scales": vsp[1],
        "offs": striped(idx),
        "offs2": striped8(idx2),
        "offs3": striped8(idx3),
        "offs4": striped(idx4),
        "offs5": striped8(idx5),
        "offs6": striped8(idx6),
        "offs7": striped8(idx7),
    }


def reference(xt_words, xt_scales, w_words, w_scales, w2_words, w2_scales, sa, vs_words, vs_scales, offs, offs2, offs3, offs4, offs5, offs6, offs7):
    idx = unstriped(offs)
    idx2 = unstriped8(offs2)
    idx3 = unstriped8(offs3)
    idx4 = unstriped(offs4)
    idx5 = unstriped8(offs5)
    idx6 = unstriped8(offs6)
    idx7 = unstriped8(offs7)
    xtu = unpack_weight(xt_words, xt_scales, "e4m3")
    wu = unpack_weight(w_words, w_scales, "e4m3")
    w2u = unpack_weight(w2_words, w2_scales, "e2m1")
    vsu = unpack_weight(vs_words, vs_scales, "e2m1")
    xtidxg = xtu[:, idx]
    a = wu.T @ xtidxg
    b = w2u.T @ xtidxg
    pw = np.zeros((R, C))
    pw[np.arange(R)[:, None], idx2[np.arange(R) % 512 // 64]] = a
    pv = np.zeros((R, C))
    pv[np.arange(R)[:, None], idx3[np.arange(R) % 512 // 64]] = b
    pg = np.sqrt(np.square(pw) + np.square(pv))
    hid = pg * f64(sa)
    vsidx4g = vsu[:, idx4]
    hidq = mxq(hid, 0, "e4m3")
    p = vsidx4g.T @ hidq
    m0 = np.zeros((N, U))
    m0[np.arange(N)[:, None], idx5[np.arange(N) % 128 // 16]] = p
    m1 = np.zeros((N, U))
    m1[np.arange(N)[:, None], idx6[np.arange(N) % 128 // 16]] = p
    m2 = np.zeros((N, U))
    m2[np.arange(N)[:, None], idx7[np.arange(N) % 128 // 16]] = p
    y = np.maximum(np.minimum(m0, m1), np.minimum(np.maximum(m0, m1), m2))
    return y

@@ -1,0 +1,262 @@
+from contextlib import ExitStack
+
+import concourse.mybir as mybir
+
+K, J, R, T, C, N, S, U = 512, 256, 512, 1024, 512, 256, 1024, 1024
+FLOPS = 2 * K * R * J * 2 + 2 * R * N * C
+
+F32 = mybir.dt.float32
+BF16 = mybir.dt.bfloat16
+I32 = mybir.dt.int32
+U32 = mybir.dt.uint32
+U16 = mybir.dt.uint16
+U8 = mybir.dt.uint8
+FP8X4 = mybir.dt.float8_e4m3fn_x4
+FP4X4 = mybir.dt.float4_e2m1fn_x4
+ACT = mybir.ActivationFunctionType
+ALU = mybir.AluOpType
+
+P = 128
+PACK = 4
+QUAD = 32
+LIST_ROWS = 16
+CHUNKS = ((0, 128), (128, 256), (256, 512))
+TAIL = ((0, 384), (384, 704), (704, 896), (896, 1024))
+
+
+def tile_picked_tokens_bare_twin_modulus_store_endmedian_kernel(
+    tc, xt_words, xt_scales, w_words, w_scales, w2_words, w2_scales, sa, vs_words, vs_scales,
+    offs, offs2, offs3, offs4, offs5, offs6, offs7, out,
+):
+    nc = tc.nc
+    with ExitStack() as ctx:
+        lists = ctx.enter_context(tc.tile_pool(name="lists", bufs=1))
+        keep = ctx.enter_context(tc.tile_pool(name="keep", bufs=1))
+        psum = ctx.enter_context(tc.psum_pool(name="psum", bufs=1))
+
+        def load_list(src, name):
+            t = lists.tile(list(src.shape), U16, name=name)
+            nc.sync.dma_start(t[:], src)
+            return t
+
+        def load_scale_rows(src, width, name):
+            t = keep.tile([PACK, PACK, width], U8, name=name, align_bytes=64)
+            nc.sync.dma_start(t[:].bitcast(I32), src[0].rearrange("(q i) c -> i q c", i=PACK).bitcast(I32))
+            return t
+
+        def load_words(src2d, width, dtype, name):
+            t = keep.tile([P, width], dtype, name=name, tag=name, align_bytes=64)
+            nc.sync.dma_start(t[:].bitcast(I32), src2d.bitcast(I32))
+            return t
+
+        def zeros(width, dtype, name, tag=""):
+            t = keep.tile([P, width], dtype, name=name, tag=tag or name, align_bytes=64)
+            if dtype == U8:
+                nc.vector.memset(t[:].bitcast(I32), 0)
+            else:
+                nc.vector.memset(t[:], 0.0)
+            return t
+
+        def spread(plane, rows):
+            for q in range(PACK):
+                nc.vector.tensor_copy(
+                    out=plane[QUAD * q : QUAD * q + PACK, :].bitcast(I32), in_=rows[:, q, :].bitcast(I32)
+                )
+
+        w2_rows = load_scale_rows(w2_scales, R, "w2_rows")
+        l_tok = load_list(offs, "l_tok")
+        xt_plane = keep.tile([P, T], U8, name="xt_plane", align_bytes=64)
+        for q in range(PACK):
+            rows = xt_scales[0, PACK * q : PACK * (q + 1), :].bitcast(I32)
+            nc.sync.dma_start(
+                xt_plane[QUAD * q : QUAD * (q + 1), :].bitcast(I32),
+                rows.unsqueeze(0).to_broadcast([QUAD // PACK, PACK, T // PACK]),
+            )
+        w2_raw = load_words(w2_words[0], R, U16, "w2_raw")
+        xt_win = load_words(xt_words[0].rearrange("p c r -> p (c r)"), T, U32, "xt_win")
+        l_pv = load_list(offs3, "l_pv")
+        w_rows = load_scale_rows(w_scales, R, "w_rows")
+        w_raw = load_words(w_words[0].rearrange("p c r -> p (c r)"), R, U32, "w_raw")
+        l_pw = load_list(offs2, "l_pw")
+        vs_rows = load_scale_rows(vs_scales, S, "vs_rows")
+        l_ent = load_list(offs4, "l_ent")
+        vs_win = load_words(vs_words[0], S, U16, "vs_win")
+        sa_sb = keep.tile([P, PACK], F32, name="sa_sb")
+        nc.sync.dma_start(sa_sb[:], sa.rearrange("(p t) o -> p (t o)", t=PACK))
+        l_page = [load_list(src, "l_page%d" % i) for i, src in enumerate((offs5, offs6, offs7))]
+
+        w2_plane = zeros(R, U8, "w2_plane")
+        pv = [zeros(C, F32, "pv%d" % i) for i in range(2)]
+        w_plane = zeros(R, U8, "w_plane")
+        vs_plane = zeros(S, U8, "vs_plane")
+        pw = [zeros(C, F32, "pw%d" % i) for i in range(2)]
+
+        def deal(engine_copy, dst, raw, t0, t1):
+            engine_copy(out=dst[:, t0:t1, :], in_=raw[:].rearrange("p (m t) -> p t m", t=PACK)[:, t0:t1, :])
+
+        w2_scale = keep.tile([P, PACK, P], U8, name="w2_scale", align_bytes=64)
+        w2_code = keep.tile([P, PACK, P], U16, name="w2_code", align_bytes=64)
+        w_scale = keep.tile([P, PACK, P], U8, name="w_scale", align_bytes=64)
+        w_code = keep.tile([P, PACK, P], U32, name="w_code", align_bytes=64)
+        xg_scale = keep.tile([P, J], U8, name="xg_scale", align_bytes=64)
+        xg_code = keep.tile([P, J], U32, name="xg_code", align_bytes=64)
+        half = J // 2
+
+        spread(w2_plane, w2_rows)
+        deal(nc.vector.tensor_copy, w2_scale, w2_plane, 0, 2)
+        nc.vector.tensor_copy(out=xg_scale[:], in_=xt_plane[:].indirect(l_tok[:]))
+        deal(nc.scalar.copy, w2_code, w2_raw, 0, PACK)
+        for h in range(2):
+            nc.vector.tensor_copy(
+                out=xg_code[:, half * h : half * (h + 1)],
+                in_=xt_win[:].indirect(l_tok[:, half * h // LIST_ROWS : half * (h + 1) // LIST_ROWS]),
+            )
+
+        def first_product(dst, code, fmt, scale, t, lo, hi):
+            nc.tensor.matmul_mx(
+                out=dst, lhsT=code[:, t, :].bitcast(fmt), lhsT_scale=scale[:, t, :],
+                rhs=xg_code[:, lo:hi].bitcast(FP8X4), rhs_scale=xg_scale[:, lo:hi], start=True, stop=True,
+            )
+
+        def product_b(dst, t, lo=0, hi=J):
+            first_product(dst, w2_code, FP4X4, w2_scale, t, lo, hi)
+
+        def product_a(dst, t):
+            first_product(dst, w_code, FP8X4, w_scale, t, 0, J)
+
+        sq_b = keep.tile([P, PACK, J], F32, name="sq_b")
+        sq_a = keep.tile([P, PACK, J], F32, name="sq_a")
+        ssum = keep.tile([P, PACK, C], F32, name="ssum")
+
+        def square(dst, bank, tag):
+            held = keep.tile(list(bank.shape), F32, name=tag, tag=tag, align_bytes=64)
+            nc.vector.tensor_copy(out=held[:], in_=bank)
+            nc.vector.tensor_tensor(out=dst, in0=bank, in1=held[:], op=ALU.mult)
+
+        def put_b(t, lo=0, hi=J):
+            nc.scalar.activation(
+                out=pv[t % 2][:].indirect(l_pv[:, lo // LIST_ROWS : hi // LIST_ROWS]), in_=sq_b[:, t, lo:hi], func=ACT.Copy
+            )
+
+        def put_a(t):
+            nc.scalar.activation(out=pw[t % 2][:].indirect(l_pw[:]), in_=sq_a[:, t, :], func=ACT.Copy)
+
+        def add_boards(t, lo, hi):
+            nc.vector.tensor_tensor(
+                out=ssum[:, t, lo:hi], in0=pv[t % 2][:, lo:hi], in1=pw[t % 2][:, lo:hi], op=ALU.add
+            )
+
+        bank = psum.tile([P, half], F32, name="b0_first", tag="bank0")
+        product_b(bank[:], 0, 0, half)
+        nc.scalar.activation(out=sq_b[:, 0, 0:half], in_=bank[:], func=ACT.Square)
+        put_b(0, 0, half)
+        bank = psum.tile([P, half], F32, name="b0_second", tag="bank1")
+        product_b(bank[:], 0, half, J)
+        square(sq_b[:, 0, half:J], bank[:], "held0")
+        put_b(0, half, J)
+        bank = psum.tile([P, J], F32, name="b1", tag="bank2")
+        product_b(bank[:], 1)
+        square(sq_b[:, 1, :], bank[:], "held1")
+        put_b(1)
+
+        spread(w_plane, w_rows)
+        deal(nc.vector.tensor_copy, w_scale, w_plane, 0, PACK)
+        deal(nc.vector.tensor_copy, w_code, w_raw, 0, PACK)
+        deal(nc.vector.tensor_copy, w2_scale, w2_plane, 2, PACK)
+        bank = psum.tile([P, 2, J], F32, name="a01", tag="bank3")
+        product_a(bank[:, 0, :], 0)
+        product_a(bank[:, 1, :], 1)
+        square(sq_a[:, 0:2, :], bank[:], "held2")
+        put_a(0)
+        put_a(1)
+        bank_b = psum.tile([P, 2, J], F32, name="b23", tag="bank4")
+        product_b(bank_b[:, 0, :], 2)
+        product_b(bank_b[:, 1, :], 3)
+        bank_a = psum.tile([P, 2, J], F32, name="a23", tag="bank5")
+        product_a(bank_a[:, 0, :], 2)
+        product_a(bank_a[:, 1, :], 3)
+        square(sq_b[:, 2:4, :], bank_b[:], "held3")
+        add_boards(0, 0, C)
+        put_b(2)
+        square(sq_a[:, 2:4, :], bank_a[:], "held4")
+        put_a(2)
+        add_boards(1, 0, C)
+        put_b(3)
+        put_a(3)
+
+        spread(vs_plane, vs_rows)
+        vg_scale = keep.tile([P, N], U8, name="vg_scale", align_bytes=64)
+        nc.vector.tensor_copy(out=vg_scale[:], in_=vs_plane[:].indirect(l_ent[:]))
+        vg_code = keep.tile([P, N], U16, name="vg_code", align_bytes=64)
+        nc.vector.tensor_copy(out=vg_code[:], in_=vs_win[:].indirect(l_ent[:]))
+        page0 = [zeros(U, F32, "page0_0", "held2"), zeros(U, F32, "page0_1", "held4")]
+        page1 = zeros(U, F32, "page1", "held3")
+        page2 = zeros(U, F32, "page2", "held1")
+        add_boards(2, 0, C)
+
+        pg = keep.tile([P, PACK, C], F32, name="pg")
+        hid = keep.tile([P, C, PACK], BF16, name="hid", align_bytes=64)
+        h_code = keep.tile([P, C], U32, name="h_code", align_bytes=64)
+        h_scale = keep.tile([P, C], U8, name="h_scale", align_bytes=64)
+        p_sb = [keep.tile([P, C], F32, name="p_sb%d" % b) for b in range(2)]
+
+        def second_product(dst, b, lo, hi):
+            nc.tensor.matmul_mx(
+                out=dst, lhsT=vg_code[:, P * b : P * (b + 1)].bitcast(FP4X4), lhsT_scale=vg_scale[:, P * b : P * (b + 1)],
+                rhs=h_code[:, lo:hi].bitcast(FP8X4), rhs_scale=h_scale[:, lo:hi], start=True, stop=True,
+            )
+
+        def put(page, which, b, lo, hi):
+            nc.scalar.activation(
+                out=page[:].indirect(l_page[which][:, lo // LIST_ROWS : hi // LIST_ROWS]),
+                in_=p_sb[b][:, lo:hi], func=ACT.Copy,
+            )
+
+        for lo, hi in CHUNKS:
+            add_boards(PACK - 1, lo, hi)
+        for lo, hi in CHUNKS:
+            nc.scalar.activation(out=pg[:, :, lo:hi], in_=ssum[:, :, lo:hi], func=ACT.Sqrt)
+        for i, (lo, hi) in enumerate(CHUNKS):
+            nc.vector.tensor_tensor(
+                out=hid[:, lo:hi, :].rearrange("p (g e) t -> p g t e", e=PACK),
+                in0=pg[:, :, lo:hi].rearrange("p t (g e) -> p g t e", e=PACK),
+                in1=sa_sb[:].unsqueeze(1).unsqueeze(3).to_broadcast([P, (hi - lo) // PACK, PACK, PACK]),
+                op=ALU.mult,
+            )
+            nc.vector.quantize_mx(
+                out=h_code[:, lo:hi].bitcast(FP8X4), scales=h_scale[:, lo:hi],
+                in_=hid[:, lo:hi, :].rearrange("p c t -> p (c t)"),
+            )
+            bank = psum.tile([P, hi - lo], F32, name="bank_p%d" % i, tag="bank%d" % ((6 + i) % 8))
+            second_product(bank[:], 0, lo, hi)
+            nc.vector.tensor_copy(out=p_sb[0][:, lo:hi], in_=bank[:])
+            for which, page in enumerate((page0[0], page1, page2)):
+                put(page, which, 0, lo, hi)
+        bank = psum.tile([P, C], F32, name="bank_q", tag="bank1")
+        second_product(bank[:], 1, 0, C)
+        nc.vector.tensor_copy(out=p_sb[1][:], in_=bank[:])
+
+        def median(b, pieces):
+            low = keep.tile([P, U], F32, name="low%d" % b)
+            high = keep.tile([P, U], F32, name="high%d" % b)
+            cut = keep.tile([P, U], F32, name="cut%d" % b)
+            res = keep.tile([P, U], F32, name="res%d" % b)
+            nc.vector.tensor_tensor(out=high[:], in0=page0[b][:], in1=page1[:], op=ALU.max)
+            nc.vector.tensor_tensor(out=low[:], in0=page0[b][:], in1=page1[:], op=ALU.min)
+            if b == 1:
+                put(page2, 2, 1, 0, C)
+
+            def finish(lo, hi):
+                nc.vector.tensor_tensor(out=res[:, lo:hi], in0=low[:, lo:hi], in1=cut[:, lo:hi], op=ALU.max)
+                nc.sync.dma_start(out[P * b : P * (b + 1), lo:hi], res[:, lo:hi])
+
+            for i, (lo, hi) in enumerate(pieces):
+                nc.vector.tensor_tensor(out=cut[:, lo:hi], in0=high[:, lo:hi], in1=page2[:, lo:hi], op=ALU.min)
+                if i > 0:
+                    finish(*pieces[i - 1])
+            finish(*pieces[-1])
+
+        median(0, ((0, U),))
+        put(page0[1], 0, 1, 0, C)
+        put(page1, 1, 1, 0, C)
+        median(1, TAIL)

@@ -63,6 +63,11 @@ def tile_picked_tokens_bare_twin_modulus_store_endmedian_kernel(
                     out=plane[QUAD * q : QUAD * q + PACK, :].bitcast(I32), in_=rows[:, q, :].bitcast(I32)
                 )
 
+        warm_in = keep.tile([P, 1], F32, name="warm_in")
+        warm_out = keep.tile([P, 1], F32, name="warm_out")
+        nc.gpsimd.memset(warm_in[:], 1.0)
+        nc.scalar.activation(out=warm_out[:], in_=warm_in[:], func=ACT.Sqrt)
+
         w2_rows = load_scale_rows(w2_scales, R, "w2_rows")
         l_tok = load_list(offs, "l_tok")
         xt_plane = keep.tile([P, T], U8, name="xt_plane", align_bytes=64)

@@ -34,88 +34,76 @@ def tile_picked_tokens_bare_twin_modulus_store_endmedian_kernel(
         keep = ctx.enter_context(tc.tile_pool(name="keep", bufs=1))
         psum = ctx.enter_context(tc.psum_pool(name="psum", bufs=1))
 
+        def sbuf(shape, dtype, name, tag=""):
+            return keep.tile(shape, dtype, name=name, tag=tag or name, align_bytes=64)
+
         def load_list(src, name):
             t = lists.tile(list(src.shape), U16, name=name)
             nc.sync.dma_start(t[:], src)
             return t
 
-        def load_scale_rows(src, width, name):
-            t = keep.tile([PACK, PACK, width], U8, name=name, align_bytes=64)
-            nc.sync.dma_start(t[:].bitcast(I32), src[0].rearrange("(q i) c -> i q c", i=PACK).bitcast(I32))
+        def load_plane(src, width, name, tag=""):
+            t = sbuf([P, width], U8, name, tag)
+            for q in range(PACK):
+                rows = src[0, PACK * q : PACK * (q + 1), :].bitcast(I32)
+                nc.sync.dma_start(
+                    t[QUAD * q : QUAD * (q + 1), :].bitcast(I32),
+                    rows.unsqueeze(0).to_broadcast([QUAD // PACK, PACK, width // PACK]),
+                )
             return t
 
-        def load_words(src2d, width, dtype, name):
-            t = keep.tile([P, width], dtype, name=name, tag=name, align_bytes=64)
+        def load_words(src2d, width, dtype, name, tag=""):
+            t = sbuf([P, width], dtype, name, tag)
             nc.sync.dma_start(t[:].bitcast(I32), src2d.bitcast(I32))
             return t
 
-        def zeros(width, dtype, name, tag=""):
-            t = keep.tile([P, width], dtype, name=name, tag=tag or name, align_bytes=64)
-            if dtype == U8:
-                nc.vector.memset(t[:].bitcast(I32), 0)
-            else:
-                nc.vector.memset(t[:], 0.0)
+        def zeros(width, name, tag="", engine=nc.vector):
+            t = sbuf([P, width], F32, name, tag)
+            engine.memset(t[:], 0.0)
             return t
-
-        def spread(plane, rows):
-            for q in range(PACK):
-                nc.vector.tensor_copy(
-                    out=plane[QUAD * q : QUAD * q + PACK, :].bitcast(I32), in_=rows[:, q, :].bitcast(I32)
-                )
 
         warm_in = keep.tile([P, 1], F32, name="warm_in")
         warm_out = keep.tile([P, 1], F32, name="warm_out")
-        nc.gpsimd.memset(warm_in[:], 1.0)
+        nc.vector.memset(warm_in[:], 1.0)
         nc.scalar.activation(out=warm_out[:], in_=warm_in[:], func=ACT.Sqrt)
 
-        w2_rows = load_scale_rows(w2_scales, R, "w2_rows")
+        w2_rows = sbuf([PACK, PACK, R], U8, "w2_rows")
+        nc.sync.dma_start(w2_rows[:].bitcast(I32), w2_scales[0].rearrange("(q i) c -> i q c", i=PACK).bitcast(I32))
         l_tok = load_list(offs, "l_tok")
-        xt_plane = keep.tile([P, T], U8, name="xt_plane", align_bytes=64)
-        for q in range(PACK):
-            rows = xt_scales[0, PACK * q : PACK * (q + 1), :].bitcast(I32)
-            nc.sync.dma_start(
-                xt_plane[QUAD * q : QUAD * (q + 1), :].bitcast(I32),
-                rows.unsqueeze(0).to_broadcast([QUAD // PACK, PACK, T // PACK]),
-            )
+        xt_plane = load_plane(xt_scales, T, "xt_plane")
         w2_raw = load_words(w2_words[0], R, U16, "w2_raw")
         xt_win = load_words(xt_words[0].rearrange("p c r -> p (c r)"), T, U32, "xt_win")
         l_pv = load_list(offs3, "l_pv")
-        w_rows = load_scale_rows(w_scales, R, "w_rows")
         w_raw = load_words(w_words[0].rearrange("p c r -> p (c r)"), R, U32, "w_raw")
+        w_plane = load_plane(w_scales, R, "w_plane")
         l_pw = load_list(offs2, "l_pw")
-        vs_rows = load_scale_rows(vs_scales, S, "vs_rows")
         l_ent = load_list(offs4, "l_ent")
-        vs_win = load_words(vs_words[0], S, U16, "vs_win")
-        sa_sb = keep.tile([P, PACK], F32, name="sa_sb")
+        sa_sb = sbuf([P, PACK], F32, "sa_sb")
         nc.sync.dma_start(sa_sb[:], sa.rearrange("(p t) o -> p (t o)", t=PACK))
         l_page = [load_list(src, "l_page%d" % i) for i, src in enumerate((offs5, offs6, offs7))]
 
-        w2_plane = zeros(R, U8, "w2_plane")
-        pv = [zeros(C, F32, "pv%d" % i) for i in range(2)]
-        w_plane = zeros(R, U8, "w_plane")
-        vs_plane = zeros(S, U8, "vs_plane")
-        pw = [zeros(C, F32, "pw%d" % i) for i in range(2)]
+        w2_plane = sbuf([P, R], U8, "w2_plane")
+        nc.vector.memset(w2_plane[:].bitcast(I32), 0)
 
         def deal(engine_copy, dst, raw, t0, t1):
             engine_copy(out=dst[:, t0:t1, :], in_=raw[:].rearrange("p (m t) -> p t m", t=PACK)[:, t0:t1, :])
 
-        w2_scale = keep.tile([P, PACK, P], U8, name="w2_scale", align_bytes=64)
-        w2_code = keep.tile([P, PACK, P], U16, name="w2_code", align_bytes=64)
-        w_scale = keep.tile([P, PACK, P], U8, name="w_scale", align_bytes=64)
-        w_code = keep.tile([P, PACK, P], U32, name="w_code", align_bytes=64)
-        xg_scale = keep.tile([P, J], U8, name="xg_scale", align_bytes=64)
-        xg_code = keep.tile([P, J], U32, name="xg_code", align_bytes=64)
+        w2_scale = sbuf([P, PACK, P], U8, "w2_scale")
+        w2_code = sbuf([P, PACK, P], U16, "w2_code")
+        xg_scale = sbuf([P, J], U8, "xg_scale")
+        xg_code = sbuf([P, J], U32, "xg_code")
         half = J // 2
 
-        spread(w2_plane, w2_rows)
+        def gather_tokens(dst, window, lo, hi):
+            nc.vector.tensor_copy(out=dst[:, lo:hi], in_=window[:].indirect(l_tok[:, lo // LIST_ROWS : hi // LIST_ROWS]))
+
+        for q in range(PACK):
+            nc.vector.tensor_copy(out=w2_plane[QUAD * q : QUAD * q + PACK, :].bitcast(I32), in_=w2_rows[:, q, :].bitcast(I32))
         deal(nc.vector.tensor_copy, w2_scale, w2_plane, 0, 2)
-        nc.vector.tensor_copy(out=xg_scale[:], in_=xt_plane[:].indirect(l_tok[:]))
+        gather_tokens(xg_scale, xt_plane, 0, J)
         deal(nc.scalar.copy, w2_code, w2_raw, 0, PACK)
-        for h in range(2):
-            nc.vector.tensor_copy(
-                out=xg_code[:, half * h : half * (h + 1)],
-                in_=xt_win[:].indirect(l_tok[:, half * h // LIST_ROWS : half * (h + 1) // LIST_ROWS]),
-            )
+        gather_tokens(xg_code, xt_win, 0, half)
+        gather_tokens(xg_code, xt_win, half, J)
 
         def first_product(dst, code, fmt, scale, t, lo, hi):
             nc.tensor.matmul_mx(
@@ -129,27 +117,26 @@ def tile_picked_tokens_bare_twin_modulus_store_endmedian_kernel(
         def product_a(dst, t):
             first_product(dst, w_code, FP8X4, w_scale, t, 0, J)
 
-        sq_b = keep.tile([P, PACK, J], F32, name="sq_b")
-        sq_a = keep.tile([P, PACK, J], F32, name="sq_a")
-        ssum = keep.tile([P, PACK, C], F32, name="ssum")
+        sq_b = sbuf([P, PACK, J], F32, "sq_b")
+        sq_a = sbuf([P, PACK, J], F32, "sq_a")
 
         def square(dst, bank, tag):
-            held = keep.tile(list(bank.shape), F32, name=tag, tag=tag, align_bytes=64)
+            held = sbuf(list(bank.shape), F32, tag)
             nc.vector.tensor_copy(out=held[:], in_=bank)
             nc.vector.tensor_tensor(out=dst, in0=bank, in1=held[:], op=ALU.mult)
 
+        pv, pw = {}, {}
+
         def put_b(t, lo=0, hi=J):
+            if lo == 0:
+                pv[t] = zeros(C, "pv%d" % t)
             nc.scalar.activation(
-                out=pv[t % 2][:].indirect(l_pv[:, lo // LIST_ROWS : hi // LIST_ROWS]), in_=sq_b[:, t, lo:hi], func=ACT.Copy
+                out=pv[t][:].indirect(l_pv[:, lo // LIST_ROWS : hi // LIST_ROWS]), in_=sq_b[:, t, lo:hi], func=ACT.Copy
             )
 
         def put_a(t):
-            nc.scalar.activation(out=pw[t % 2][:].indirect(l_pw[:]), in_=sq_a[:, t, :], func=ACT.Copy)
-
-        def add_boards(t, lo, hi):
-            nc.vector.tensor_tensor(
-                out=ssum[:, t, lo:hi], in0=pv[t % 2][:, lo:hi], in1=pw[t % 2][:, lo:hi], op=ALU.add
-            )
+            pw[t] = zeros(C, "pw%d" % t, ("held_b23", "w_plane", "w_raw", "w2_scale")[t], nc.gpsimd)
+            nc.scalar.activation(out=pw[t][:].indirect(l_pw[:]), in_=sq_a[:, t, :], func=ACT.Copy)
 
         bank = psum.tile([P, half], F32, name="b0_first", tag="bank0")
         product_b(bank[:], 0, 0, half)
@@ -157,53 +144,51 @@ def tile_picked_tokens_bare_twin_modulus_store_endmedian_kernel(
         put_b(0, 0, half)
         bank = psum.tile([P, half], F32, name="b0_second", tag="bank1")
         product_b(bank[:], 0, half, J)
-        square(sq_b[:, 0, half:J], bank[:], "held0")
+        square(sq_b[:, 0, half:J], bank[:], "held_b0")
         put_b(0, half, J)
         bank = psum.tile([P, J], F32, name="b1", tag="bank2")
         product_b(bank[:], 1)
-        square(sq_b[:, 1, :], bank[:], "held1")
+        square(sq_b[:, 1, :], bank[:], "held_b1")
         put_b(1)
 
-        spread(w_plane, w_rows)
+        deal(nc.vector.tensor_copy, w2_scale, w2_plane, 2, PACK)
+        bank = psum.tile([P, 2, J], F32, name="b23", tag="bank3")
+        product_b(bank[:, 0, :], 2)
+        product_b(bank[:, 1, :], 3)
+        square(sq_b[:, 2:4, :], bank[:], "held_b23")
+        put_b(2)
+        put_b(3)
+
+        w_scale = sbuf([P, PACK, P], U8, "w_scale", "held_b0")
+        w_code = sbuf([P, PACK, P], U32, "w_code", "held_b1")
         deal(nc.vector.tensor_copy, w_scale, w_plane, 0, PACK)
         deal(nc.vector.tensor_copy, w_code, w_raw, 0, PACK)
-        deal(nc.vector.tensor_copy, w2_scale, w2_plane, 2, PACK)
-        bank = psum.tile([P, 2, J], F32, name="a01", tag="bank3")
-        product_a(bank[:, 0, :], 0)
-        product_a(bank[:, 1, :], 1)
-        square(sq_a[:, 0:2, :], bank[:], "held2")
-        put_a(0)
-        put_a(1)
-        bank_b = psum.tile([P, 2, J], F32, name="b23", tag="bank4")
-        product_b(bank_b[:, 0, :], 2)
-        product_b(bank_b[:, 1, :], 3)
-        bank_a = psum.tile([P, 2, J], F32, name="a23", tag="bank5")
-        product_a(bank_a[:, 0, :], 2)
-        product_a(bank_a[:, 1, :], 3)
-        square(sq_b[:, 2:4, :], bank_b[:], "held3")
-        add_boards(0, 0, C)
-        put_b(2)
-        square(sq_a[:, 2:4, :], bank_a[:], "held4")
-        put_a(2)
-        add_boards(1, 0, C)
-        put_b(3)
-        put_a(3)
+        for pair in range(2):
+            bank = psum.tile([P, 2, J], F32, name="a_pair%d" % pair, tag="bank%d" % (4 + pair))
+            product_a(bank[:, 0, :], 2 * pair)
+            product_a(bank[:, 1, :], 2 * pair + 1)
+            square(sq_a[:, 2 * pair : 2 * pair + 2, :], bank[:], "held_a%d" % pair)
+            put_a(2 * pair)
+            put_a(2 * pair + 1)
 
-        spread(vs_plane, vs_rows)
-        vg_scale = keep.tile([P, N], U8, name="vg_scale", align_bytes=64)
+        vs_plane = load_plane(vs_scales, S, "vs_plane", "xt_plane")
+        vs_win = load_words(vs_words[0], S, U16, "vs_win", "held_a0")
+        vg_scale = sbuf([P, N], U8, "vg_scale")
         nc.vector.tensor_copy(out=vg_scale[:], in_=vs_plane[:].indirect(l_ent[:]))
-        vg_code = keep.tile([P, N], U16, name="vg_code", align_bytes=64)
+        page0 = [zeros(U, "page0_first", "held_b1", nc.gpsimd)]
+        page1 = zeros(U, "page1", "held_b0", nc.gpsimd)
+        page2 = zeros(U, "page2", "held_a1", nc.gpsimd)
+        vg_code = sbuf([P, N], U16, "vg_code")
         nc.vector.tensor_copy(out=vg_code[:], in_=vs_win[:].indirect(l_ent[:]))
-        page0 = [zeros(U, F32, "page0_0", "held2"), zeros(U, F32, "page0_1", "held4")]
-        page1 = zeros(U, F32, "page1", "held3")
-        page2 = zeros(U, F32, "page2", "held1")
-        add_boards(2, 0, C)
 
-        pg = keep.tile([P, PACK, C], F32, name="pg")
-        hid = keep.tile([P, C, PACK], BF16, name="hid", align_bytes=64)
-        h_code = keep.tile([P, C], U32, name="h_code", align_bytes=64)
-        h_scale = keep.tile([P, C], U8, name="h_scale", align_bytes=64)
-        p_sb = [keep.tile([P, C], F32, name="p_sb%d" % b) for b in range(2)]
+        ssum = sbuf([P, PACK, C], F32, "ssum", "held_a0")
+        pg = sbuf([P, PACK, C], F32, "pg")
+        h_code = sbuf([P, C], U32, "h_code")
+        h_scale = sbuf([P, C], U8, "h_scale")
+        p_sb = [sbuf([P, C], F32, "p_sb%d" % b) for b in range(2)]
+
+        def add_boards(t, lo, hi):
+            nc.vector.tensor_tensor(out=ssum[:, t, lo:hi], in0=pv[t][:, lo:hi], in1=pw[t][:, lo:hi], op=ALU.add)
 
         def second_product(dst, b, lo, hi):
             nc.tensor.matmul_mx(
@@ -217,35 +202,45 @@ def tile_picked_tokens_bare_twin_modulus_store_endmedian_kernel(
                 in_=p_sb[b][:, lo:hi], func=ACT.Copy,
             )
 
+        for t in range(PACK - 1):
+            add_boards(t, 0, C)
         for lo, hi in CHUNKS:
             add_boards(PACK - 1, lo, hi)
-        for lo, hi in CHUNKS:
+
+        lo, hi = CHUNKS[0]
+        nc.scalar.activation(out=pg[:, : PACK - 1, lo:hi], in_=ssum[:, : PACK - 1, lo:hi], func=ACT.Sqrt)
+        nc.scalar.activation(out=pg[:, PACK - 1, lo:hi], in_=ssum[:, PACK - 1, lo:hi], func=ACT.Sqrt)
+        for lo, hi in CHUNKS[1:]:
             nc.scalar.activation(out=pg[:, :, lo:hi], in_=ssum[:, :, lo:hi], func=ACT.Sqrt)
         for i, (lo, hi) in enumerate(CHUNKS):
+            hid = sbuf([P, hi - lo, PACK], BF16, "hid%d" % i, "hid")
             nc.vector.tensor_tensor(
-                out=hid[:, lo:hi, :].rearrange("p (g e) t -> p g t e", e=PACK),
+                out=hid[:].rearrange("p (g e) t -> p g t e", e=PACK),
                 in0=pg[:, :, lo:hi].rearrange("p t (g e) -> p g t e", e=PACK),
                 in1=sa_sb[:].unsqueeze(1).unsqueeze(3).to_broadcast([P, (hi - lo) // PACK, PACK, PACK]),
                 op=ALU.mult,
             )
             nc.vector.quantize_mx(
                 out=h_code[:, lo:hi].bitcast(FP8X4), scales=h_scale[:, lo:hi],
-                in_=hid[:, lo:hi, :].rearrange("p c t -> p (c t)"),
+                in_=hid[:].rearrange("p c t -> p (c t)"),
             )
-            bank = psum.tile([P, hi - lo], F32, name="bank_p%d" % i, tag="bank%d" % ((6 + i) % 8))
+            bank = psum.tile([P, hi - lo], F32, name="p_first%d" % i, tag="bank%d" % ((6 + i) % 8))
             second_product(bank[:], 0, lo, hi)
-            nc.vector.tensor_copy(out=p_sb[0][:, lo:hi], in_=bank[:])
+            leave_psum = nc.scalar.copy if i == 0 else nc.vector.tensor_copy
+            leave_psum(out=p_sb[0][:, lo:hi], in_=bank[:])
             for which, page in enumerate((page0[0], page1, page2)):
                 put(page, which, 0, lo, hi)
-        bank = psum.tile([P, C], F32, name="bank_q", tag="bank1")
+
+        bank = psum.tile([P, C], F32, name="p_second", tag="bank1")
         second_product(bank[:], 1, 0, C)
         nc.vector.tensor_copy(out=p_sb[1][:], in_=bank[:])
+        page0.append(zeros(U, "page0_second", "hid", nc.gpsimd))
 
-        def median(b, pieces):
-            low = keep.tile([P, U], F32, name="low%d" % b)
-            high = keep.tile([P, U], F32, name="high%d" % b)
-            cut = keep.tile([P, U], F32, name="cut%d" % b)
-            res = keep.tile([P, U], F32, name="res%d" % b)
+        def median(b, pieces, tags):
+            high = sbuf([P, U], F32, "high%d" % b, tags[0])
+            low = sbuf([P, U], F32, "low%d" % b, tags[1])
+            cut = sbuf([P, U], F32, "cut%d" % b)
+            res = sbuf([P, U], F32, "res%d" % b)
             nc.vector.tensor_tensor(out=high[:], in0=page0[b][:], in1=page1[:], op=ALU.max)
             nc.vector.tensor_tensor(out=low[:], in0=page0[b][:], in1=page1[:], op=ALU.min)
             if b == 1:
@@ -261,7 +256,7 @@ def tile_picked_tokens_bare_twin_modulus_store_endmedian_kernel(
                     finish(*pieces[i - 1])
             finish(*pieces[-1])
 
-        median(0, ((0, U),))
+        median(0, ((0, U),), ("high0", "low0"))
         put(page0[1], 0, 1, 0, C)
         put(page1, 1, 1, 0, C)
-        median(1, TAIL)
+        median(1, TAIL, ("cut0", "low0"))

@@ -101,7 +101,8 @@ def tile_picked_tokens_bare_twin_modulus_store_endmedian_kernel(
             nc.vector.tensor_copy(out=w2_plane[QUAD * q : QUAD * q + PACK, :].bitcast(I32), in_=w2_rows[:, q, :].bitcast(I32))
         deal(nc.vector.tensor_copy, w2_scale, w2_plane, 0, 2)
         gather_tokens(xg_scale, xt_plane, 0, J)
-        deal(nc.scalar.copy, w2_code, w2_raw, 0, PACK)
+        deal(nc.scalar.copy, w2_code, w2_raw, 0, 1)
+        deal(nc.scalar.copy, w2_code, w2_raw, 1, PACK)
         gather_tokens(xg_code, xt_win, 0, half)
         gather_tokens(xg_code, xt_win, half, J)
 
@@ -213,17 +214,18 @@ def tile_picked_tokens_bare_twin_modulus_store_endmedian_kernel(
         for lo, hi in CHUNKS[1:]:
             nc.scalar.activation(out=pg[:, :, lo:hi], in_=ssum[:, :, lo:hi], func=ACT.Sqrt)
         for i, (lo, hi) in enumerate(CHUNKS):
-            hid = sbuf([P, hi - lo, PACK], BF16, "hid%d" % i, "hid")
-            nc.vector.tensor_tensor(
-                out=hid[:].rearrange("p (g e) t -> p g t e", e=PACK),
-                in0=pg[:, :, lo:hi].rearrange("p t (g e) -> p g t e", e=PACK),
-                in1=sa_sb[:].unsqueeze(1).unsqueeze(3).to_broadcast([P, (hi - lo) // PACK, PACK, PACK]),
-                op=ALU.mult,
-            )
-            nc.vector.quantize_mx(
-                out=h_code[:, lo:hi].bitcast(FP8X4), scales=h_scale[:, lo:hi],
-                in_=hid[:].rearrange("p c t -> p (c t)"),
-            )
+            for c0 in range(lo, hi, P):
+                hid = sbuf([P, P, PACK], BF16, "hid%d" % c0, "hid")
+                nc.vector.tensor_tensor(
+                    out=hid[:].rearrange("p (g e) t -> p g t e", e=PACK),
+                    in0=pg[:, :, c0 : c0 + P].rearrange("p t (g e) -> p g t e", e=PACK),
+                    in1=sa_sb[:].unsqueeze(1).unsqueeze(3).to_broadcast([P, P // PACK, PACK, PACK]),
+                    op=ALU.mult,
+                )
+                nc.vector.quantize_mx(
+                    out=h_code[:, c0 : c0 + P].bitcast(FP8X4), scales=h_scale[:, c0 : c0 + P],
+                    in_=hid[:].rearrange("p c t -> p (c t)"),
+                )
             bank = psum.tile([P, hi - lo], F32, name="p_first%d" % i, tag="bank%d" % ((6 + i) % 8))
             second_product(bank[:], 0, lo, hi)
             leave_psum = nc.scalar.copy if i == 0 else nc.vector.tensor_copy

from contextlib import ExitStack

import concourse.mybir as mybir

K, J, R, T, C, N, S, U = 512, 256, 512, 1024, 512, 256, 1024, 1024
FLOPS = 2 * K * R * J * 2 + 2 * R * N * C

F32 = mybir.dt.float32
BF16 = mybir.dt.bfloat16
I32 = mybir.dt.int32
U32 = mybir.dt.uint32
U16 = mybir.dt.uint16
U8 = mybir.dt.uint8
FP8X4 = mybir.dt.float8_e4m3fn_x4
FP4X4 = mybir.dt.float4_e2m1fn_x4
ACT = mybir.ActivationFunctionType
ALU = mybir.AluOpType

P = 128
PACK = 4
QUAD = 32
LIST_ROWS = 16
CHUNKS = ((0, 128), (128, 256), (256, 512))
TAIL = ((0, 384), (384, 704), (704, 896), (896, 1024))


def tile_picked_tokens_bare_twin_modulus_store_endmedian_kernel(
    tc, xt_words, xt_scales, w_words, w_scales, w2_words, w2_scales, sa, vs_words, vs_scales,
    offs, offs2, offs3, offs4, offs5, offs6, offs7, out,
):
    nc = tc.nc
    with ExitStack() as ctx:
        lists = ctx.enter_context(tc.tile_pool(name="lists", bufs=1))
        keep = ctx.enter_context(tc.tile_pool(name="keep", bufs=1))
        psum = ctx.enter_context(tc.psum_pool(name="psum", bufs=1))

        def sbuf(shape, dtype, name, tag=""):
            return keep.tile(shape, dtype, name=name, tag=tag or name, align_bytes=64)

        def load_list(src, name):
            t = lists.tile(list(src.shape), U16, name=name)
            nc.sync.dma_start(t[:], src)
            return t

        def load_plane(src, width, name, tag=""):
            t = sbuf([P, width], U8, name, tag)
            for q in range(PACK):
                rows = src[0, PACK * q : PACK * (q + 1), :].bitcast(I32)
                nc.sync.dma_start(
                    t[QUAD * q : QUAD * (q + 1), :].bitcast(I32),
                    rows.unsqueeze(0).to_broadcast([QUAD // PACK, PACK, width // PACK]),
                )
            return t

        def load_words(src2d, width, dtype, name, tag=""):
            t = sbuf([P, width], dtype, name, tag)
            nc.sync.dma_start(t[:].bitcast(I32), src2d.bitcast(I32))
            return t

        def zeros(width, name, tag="", engine=nc.vector):
            t = sbuf([P, width], F32, name, tag)
            engine.memset(t[:], 0.0)
            return t

        warm_in = keep.tile([P, 1], F32, name="warm_in")
        warm_out = keep.tile([P, 1], F32, name="warm_out")
        nc.vector.memset(warm_in[:], 1.0)
        nc.scalar.activation(out=warm_out[:], in_=warm_in[:], func=ACT.Sqrt)

        w2_rows = sbuf([PACK, PACK, R], U8, "w2_rows")
        nc.sync.dma_start(w2_rows[:].bitcast(I32), w2_scales[0].rearrange("(q i) c -> i q c", i=PACK).bitcast(I32))
        l_tok = load_list(offs, "l_tok")
        xt_plane = load_plane(xt_scales, T, "xt_plane")
        w2_raw = load_words(w2_words[0], R, U16, "w2_raw")
        xt_win = load_words(xt_words[0].rearrange("p c r -> p (c r)"), T, U32, "xt_win")
        l_pv = load_list(offs3, "l_pv")
        w_raw = load_words(w_words[0].rearrange("p c r -> p (c r)"), R, U32, "w_raw")
        w_plane = load_plane(w_scales, R, "w_plane")
        l_pw = load_list(offs2, "l_pw")
        l_ent = load_list(offs4, "l_ent")
        sa_sb = sbuf([P, PACK], F32, "sa_sb")
        nc.sync.dma_start(sa_sb[:], sa.rearrange("(p t) o -> p (t o)", t=PACK))
        l_page = [load_list(src, "l_page%d" % i) for i, src in enumerate((offs5, offs6, offs7))]

        w2_plane = sbuf([P, R], U8, "w2_plane")
        nc.vector.memset(w2_plane[:].bitcast(I32), 0)

        def deal(engine_copy, dst, raw, t0, t1):
            engine_copy(out=dst[:, t0:t1, :], in_=raw[:].rearrange("p (m t) -> p t m", t=PACK)[:, t0:t1, :])

        w2_scale = sbuf([P, PACK, P], U8, "w2_scale")
        w2_code = sbuf([P, PACK, P], U16, "w2_code")
        xg_scale = sbuf([P, J], U8, "xg_scale")
        xg_code = sbuf([P, J], U32, "xg_code")
        half = J // 2

        def gather_tokens(dst, window, lo, hi):
            nc.vector.tensor_copy(out=dst[:, lo:hi], in_=window[:].indirect(l_tok[:, lo // LIST_ROWS : hi // LIST_ROWS]))

        for q in range(PACK):
            nc.vector.tensor_copy(out=w2_plane[QUAD * q : QUAD * q + PACK, :].bitcast(I32), in_=w2_rows[:, q, :].bitcast(I32))
        deal(nc.vector.tensor_copy, w2_scale, w2_plane, 0, 2)
        gather_tokens(xg_scale, xt_plane, 0, J)
        deal(nc.scalar.copy, w2_code, w2_raw, 0, 1)
        deal(nc.scalar.copy, w2_code, w2_raw, 1, PACK)
        gather_tokens(xg_code, xt_win, 0, half)
        gather_tokens(xg_code, xt_win, half, J)

        def first_product(dst, code, fmt, scale, t, lo, hi):
            nc.tensor.matmul_mx(
                out=dst, lhsT=code[:, t, :].bitcast(fmt), lhsT_scale=scale[:, t, :],
                rhs=xg_code[:, lo:hi].bitcast(FP8X4), rhs_scale=xg_scale[:, lo:hi], start=True, stop=True,
            )

        def product_b(dst, t, lo=0, hi=J):
            first_product(dst, w2_code, FP4X4, w2_scale, t, lo, hi)

        def product_a(dst, t):
            first_product(dst, w_code, FP8X4, w_scale, t, 0, J)

        sq_b = sbuf([P, PACK, J], F32, "sq_b")
        sq_a = sbuf([P, PACK, J], F32, "sq_a")

        def square(dst, bank, tag):
            held = sbuf(list(bank.shape), F32, tag)
            nc.vector.tensor_copy(out=held[:], in_=bank)
            nc.vector.tensor_tensor(out=dst, in0=bank, in1=held[:], op=ALU.mult)

        pv, pw = {}, {}

        def put_b(t, lo=0, hi=J):
            if lo == 0:
                pv[t] = zeros(C, "pv%d" % t)
            nc.scalar.activation(
                out=pv[t][:].indirect(l_pv[:, lo // LIST_ROWS : hi // LIST_ROWS]), in_=sq_b[:, t, lo:hi], func=ACT.Copy
            )

        def put_a(t):
            pw[t] = zeros(C, "pw%d" % t, ("held_b23", "w_plane", "w_raw", "w2_scale")[t], nc.gpsimd)
            nc.scalar.activation(out=pw[t][:].indirect(l_pw[:]), in_=sq_a[:, t, :], func=ACT.Copy)

        bank = psum.tile([P, half], F32, name="b0_first", tag="bank0")
        product_b(bank[:], 0, 0, half)
        nc.scalar.activation(out=sq_b[:, 0, 0:half], in_=bank[:], func=ACT.Square)
        put_b(0, 0, half)
        bank = psum.tile([P, half], F32, name="b0_second", tag="bank1")
        product_b(bank[:], 0, half, J)
        square(sq_b[:, 0, half:J], bank[:], "held_b0")
        put_b(0, half, J)
        bank = psum.tile([P, J], F32, name="b1", tag="bank2")
        product_b(bank[:], 1)
        square(sq_b[:, 1, :], bank[:], "held_b1")
        put_b(1)

        deal(nc.vector.tensor_copy, w2_scale, w2_plane, 2, PACK)
        bank = psum.tile([P, 2, J], F32, name="b23", tag="bank3")
        product_b(bank[:, 0, :], 2)
        product_b(bank[:, 1, :], 3)
        square(sq_b[:, 2:4, :], bank[:], "held_b23")
        put_b(2)
        put_b(3)

        w_scale = sbuf([P, PACK, P], U8, "w_scale", "held_b0")
        w_code = sbuf([P, PACK, P], U32, "w_code", "held_b1")
        deal(nc.vector.tensor_copy, w_scale, w_plane, 0, PACK)
        deal(nc.vector.tensor_copy, w_code, w_raw, 0, PACK)
        for pair in range(2):
            bank = psum.tile([P, 2, J], F32, name="a_pair%d" % pair, tag="bank%d" % (4 + pair))
            product_a(bank[:, 0, :], 2 * pair)
            product_a(bank[:, 1, :], 2 * pair + 1)
            square(sq_a[:, 2 * pair : 2 * pair + 2, :], bank[:], "held_a%d" % pair)
            put_a(2 * pair)
            put_a(2 * pair + 1)

        vs_plane = load_plane(vs_scales, S, "vs_plane", "xt_plane")
        vs_win = load_words(vs_words[0], S, U16, "vs_win", "held_a0")
        vg_scale = sbuf([P, N], U8, "vg_scale")
        nc.vector.tensor_copy(out=vg_scale[:], in_=vs_plane[:].indirect(l_ent[:]))
        page0 = [zeros(U, "page0_first", "held_b1", nc.gpsimd)]
        page1 = zeros(U, "page1", "held_b0", nc.gpsimd)
        page2 = zeros(U, "page2", "held_a1", nc.gpsimd)
        vg_code = sbuf([P, N], U16, "vg_code")
        nc.vector.tensor_copy(out=vg_code[:], in_=vs_win[:].indirect(l_ent[:]))

        ssum = sbuf([P, PACK, C], F32, "ssum", "held_a0")
        pg = sbuf([P, PACK, C], F32, "pg")
        h_code = sbuf([P, C], U32, "h_code")
        h_scale = sbuf([P, C], U8, "h_scale")
        p_sb = [sbuf([P, C], F32, "p_sb%d" % b) for b in range(2)]

        def add_boards(t, lo, hi):
            nc.vector.tensor_tensor(out=ssum[:, t, lo:hi], in0=pv[t][:, lo:hi], in1=pw[t][:, lo:hi], op=ALU.add)

        def second_product(dst, b, lo, hi):
            nc.tensor.matmul_mx(
                out=dst, lhsT=vg_code[:, P * b : P * (b + 1)].bitcast(FP4X4), lhsT_scale=vg_scale[:, P * b : P * (b + 1)],
                rhs=h_code[:, lo:hi].bitcast(FP8X4), rhs_scale=h_scale[:, lo:hi], start=True, stop=True,
            )

        def put(page, which, b, lo, hi):
            nc.scalar.activation(
                out=page[:].indirect(l_page[which][:, lo // LIST_ROWS : hi // LIST_ROWS]),
                in_=p_sb[b][:, lo:hi], func=ACT.Copy,
            )

        for t in range(PACK - 1):
            add_boards(t, 0, C)
        for lo, hi in CHUNKS:
            add_boards(PACK - 1, lo, hi)

        lo, hi = CHUNKS[0]
        nc.scalar.activation(out=pg[:, : PACK - 1, lo:hi], in_=ssum[:, : PACK - 1, lo:hi], func=ACT.Sqrt)
        nc.scalar.activation(out=pg[:, PACK - 1, lo:hi], in_=ssum[:, PACK - 1, lo:hi], func=ACT.Sqrt)
        for lo, hi in CHUNKS[1:]:
            nc.scalar.activation(out=pg[:, :, lo:hi], in_=ssum[:, :, lo:hi], func=ACT.Sqrt)
        for i, (lo, hi) in enumerate(CHUNKS):
            for c0 in range(lo, hi, P):
                hid = sbuf([P, P, PACK], BF16, "hid%d" % c0, "hid")
                nc.vector.tensor_tensor(
                    out=hid[:].rearrange("p (g e) t -> p g t e", e=PACK),
                    in0=pg[:, :, c0 : c0 + P].rearrange("p t (g e) -> p g t e", e=PACK),
                    in1=sa_sb[:].unsqueeze(1).unsqueeze(3).to_broadcast([P, P // PACK, PACK, PACK]),
                    op=ALU.mult,
                )
                nc.vector.quantize_mx(
                    out=h_code[:, c0 : c0 + P].bitcast(FP8X4), scales=h_scale[:, c0 : c0 + P],
                    in_=hid[:].rearrange("p c t -> p (c t)"),
                )
            bank = psum.tile([P, hi - lo], F32, name="p_first%d" % i, tag="bank%d" % ((6 + i) % 8))
            second_product(bank[:], 0, lo, hi)
            leave_psum = nc.scalar.copy if i == 0 else nc.vector.tensor_copy
            leave_psum(out=p_sb[0][:, lo:hi], in_=bank[:])
            for which, page in enumerate((page0[0], page1, page2)):
                put(page, which, 0, lo, hi)

        bank = psum.tile([P, C], F32, name="p_second", tag="bank1")
        second_product(bank[:], 1, 0, C)
        nc.vector.tensor_copy(out=p_sb[1][:], in_=bank[:])
        page0.append(zeros(U, "page0_second", "hid", nc.gpsimd))

        def median(b, pieces, tags):
            high = sbuf([P, U], F32, "high%d" % b, tags[0])
            low = sbuf([P, U], F32, "low%d" % b, tags[1])
            cut = sbuf([P, U], F32, "cut%d" % b)
            res = sbuf([P, U], F32, "res%d" % b)
            nc.vector.tensor_tensor(out=high[:], in0=page0[b][:], in1=page1[:], op=ALU.max)
            nc.vector.tensor_tensor(out=low[:], in0=page0[b][:], in1=page1[:], op=ALU.min)
            if b == 1:
                put(page2, 2, 1, 0, C)

            def finish(lo, hi):
                nc.vector.tensor_tensor(out=res[:, lo:hi], in0=low[:, lo:hi], in1=cut[:, lo:hi], op=ALU.max)
                nc.sync.dma_start(out[P * b : P * (b + 1), lo:hi], res[:, lo:hi])

            for i, (lo, hi) in enumerate(pieces):
                nc.vector.tensor_tensor(out=cut[:, lo:hi], in0=high[:, lo:hi], in1=page2[:, lo:hi], op=ALU.min)
                if i > 0:
                    finish(*pieces[i - 1])
            finish(*pieces[-1])

        median(0, ((0, U),), ("high0", "low0"))
        put(page0[1], 0, 1, 0, C)
        put(page1, 1, 1, 0, C)
        median(1, TAIL, ("cut0", "low0"))
